import numpy as np
import ml_dtypes


def mxq(x, axis, fmt="e4m3"):
    dtype, down = {"e4m3": (ml_dtypes.float8_e4m3fn, 7), "e5m2": (ml_dtypes.float8_e5m2, 14)}[fmt]
    v = np.moveaxis(np.asarray(x, np.float32).astype(ml_dtypes.bfloat16).astype(np.float64), axis, -1)
    blocks = v.reshape(v.shape[:-1] + (-1, 32))
    amax = np.abs(blocks).max(-1, keepdims=True)
    byte = np.maximum(np.where(amax > 0, np.frexp(amax)[1] - 1 + 127, 0) - down, 1)
    scale = np.exp2(byte - 127.0)
    codes = (blocks / scale).astype(np.float32).astype(dtype).astype(np.float64)
    return np.moveaxis((codes * scale).reshape(v.shape), -1, axis)


WIDE = False


def mx_kscale(k):
    if not WIDE:
        return np.ones(k)
    levels = np.array([10, -10, 5, -5, 0])
    if k % 512:
        return np.exp2(np.random.permutation(np.resize(levels, k // 32))).repeat(32)
    a = np.empty((k // 512, 16))
    for p in range(k // 512):
        a[p, :8] = np.random.permutation(np.resize(levels, 8))
        for g in range(8):
            far = levels[np.abs(levels - a[p, g]) >= 10]
            a[p, g + 8] = far[np.random.randint(len(far))]
    return np.exp2(a.ravel()).repeat(32)


def f64(x):
    return np.asarray(x).astype(np.float64)


def striped(idx):
    return np.tile(np.asarray(idx).reshape(-1, 16).T, (8, 1)).astype(np.uint16)


def unstriped(offs):
    return offs[:16].T.reshape(-1).astype(np.int64)


def striped8(idx):
    return np.asarray(idx).reshape(8, -1, 16).transpose(0, 2, 1).reshape(128, -1).astype(np.uint16)


def unstriped8(offs):
    return offs.reshape(8, 16, -1).transpose(0, 2, 1).reshape(8, -1).astype(np.int64)


def pick8(x, idx, run):
    r = np.arange(len(x))
    return x[r[:, None], idx[r % (8 * run) // run]]


E2M1 = np.array([0.0, 0.5, 1.0, 1.5, 2.0, 3.0, 4.0, 6.0, -0.0, -0.5, -1.0, -1.5, -2.0, -3.0, -4.0, -6.0])


def pack_weight(w, fmt):
    k, n = w.shape
    w = f64(np.asarray(w, np.float32).astype(ml_dtypes.bfloat16)).reshape(k // 32, 32, n)
    amax = np.abs(w).max(1)
    if fmt == "e4m3":
        byte = np.frexp(amax)[1] - 1 + 127 - 7
    else:
        mant, ex = np.frexp(amax / 6.0)
        byte = np.where(mant > 0.5, ex, ex - 1) + 127
    byte = np.clip(np.where(amax > 0, byte, 1), 1, 254)
    scaled = (w * np.exp2(127.0 - byte)[:, None, :]).reshape(k, n).astype(np.float32)
    by_word = np.ascontiguousarray(scaled.reshape(k // 512, 128, 4, n).transpose(0, 1, 3, 2))
    if fmt == "e4m3":
        words = by_word.astype(ml_dtypes.float8_e4m3fn).view(np.uint8)
    else:
        c = by_word.astype(ml_dtypes.float4_e2m1fn).view(np.uint8) & 0xF
        words = (c[..., 0::2] | (c[..., 1::2] << 4)).reshape(k // 512, 128, 2 * n)
    return np.ascontiguousarray(words), np.ascontiguousarray(byte.astype(np.uint8).reshape(k // 512, 16, n))


def unpack_weight(words, scales, fmt):
    g, _, n = scales.shape
    words = np.ascontiguousarray(words).reshape(g, 128, n, -1)
    if fmt == "e4m3":
        vals = words.view(ml_dtypes.float8_e4m3fn).astype(np.float64)
    else:
        nib = np.empty((g, 128, n, 4), np.uint8)
        nib[..., 0::2] = words & 0xF
        nib[..., 1::2] = words >> 4
        vals = E2M1[nib]
    vals = vals * np.repeat(np.exp2(scales.astype(np.float64) - 127.0), 8, axis=1)[..., None]
    return vals.transpose(0, 1, 3, 2).reshape(g * 512, n)


def sigmoid(v):
    return 1.0 / (1.0 + np.exp(-v))


K, R, F, T, J, U, M = 512, 128, 512, 2048, 512, 1024, 256


def setup_inputs():
    n = np.random.standard_normal
    idx = np.random.permutation(T)[:J]
    idx2 = np.stack([np.random.permutation(U)[:J] for _ in range(8)])
    idx3 = np.stack([np.random.permutation(U)[:M] for _ in range(8)])
    fk = mx_kscale(K)
    dtabp = pack_weight(n((K, T)) / fk[:, None], "e2m1")
    tabp = pack_weight(n((K, T)) / fk[:, None], "e2m1")
    return {
        "dtab_words": dtabp[0],
        "dtab_scales": dtabp[1],
        "tab_words": tabp[0],
        "tab_scales": tabp[1],
        "w1": (n((K, R)) * 1 / np.sqrt(K) * fk[:, None]).astype(np.float32),
        "gain": (np.random.uniform(0.5, 1.5, (R, 1))).astype(np.float32),
        "pb": (np.random.uniform(0.3, 1.0, (1, M))).astype(np.float32),
        "og": (np.random.uniform(0.5, 2.0, (R, 1))).astype(np.float32),
        "base": (0.3 * n((R, M))).astype(np.float32),
        "offs": striped(idx),
        "offs2": striped8(idx2),
        "offs3": striped8(idx3),
    }


def reference(dtab_words, dtab_scales, tab_words, tab_scales, w1, gain, pb, og, base, offs, offs2, offs3):
    idx = unstriped(offs)
    idx2 = unstriped8(offs2)
    idx3 = unstriped8(offs3)
    dtabu = unpack_weight(dtab_words, dtab_scales, "e2m1")
    tabu = unpack_weight(tab_words, tab_scales, "e2m1")
    w1q = mxq(f64(w1), 0, "e4m3")
    tabidxg = tabu[:, idx]
    a = w1q.T @ tabidxg
    dtabidxg = dtabu[:, idx]
    ta = w1q.T @ dtabidxg
    h1 = np.tanh(a)
    h2 = h1 * f64(gain)
    pg = np.zeros((R, U))
    pg[np.arange(R)[:, None], idx2[np.arange(R) % 128 // 16]] = h2
    s = pick8(pg, idx3, 16) + f64(pb)
    th1 = ta * (1.0 - np.square(h1))
    th2 = th1 * f64(gain)
    tpg = np.zeros((R, U))
    tpg[np.arange(R)[:, None], idx2[np.arange(R) % 128 // 16]] = th2
    ts = pick8(tpg, idx3, 16)
    tu1 = ts * sigmoid(s) + ts * sigmoid(s) * (1.0 - sigmoid(s)) * s
    y = tu1 * f64(og) + f64(base)
    return y

@@ -1,0 +1,122 @@
+from contextlib import ExitStack
+
+import concourse.mybir as mybir
+
+F32 = mybir.dt.float32
+BF16 = mybir.dt.bfloat16
+I32 = mybir.dt.int32
+U32 = mybir.dt.uint32
+U16 = mybir.dt.uint16
+U8 = mybir.dt.uint8
+FP8X4 = mybir.dt.float8_e4m3fn_x4
+FP4X4 = mybir.dt.float4_e2m1fn_x4
+ALU = mybir.AluOpType
+ACT = mybir.ActivationFunctionType
+
+P = 128
+PACK = 4
+K, R, T, J, U, M = 512, 128, 2048, 512, 1024, 256
+FLOPS = 2 * 2 * K * R * J
+
+
+def tile_attend_twriteread_kernel(tc, dtab_words, dtab_scales, tab_words, tab_scales, w1, gain, pb, og, base,
+                                   offs, offs2, offs3, out):
+    nc = tc.nc
+    with ExitStack() as ctx:
+        sb = ctx.enter_context(tc.tile_pool(name="sb", bufs=1))
+        psum = ctx.enter_context(tc.psum_pool(name="psum", bufs=1))
+
+        def load_words(name, words):
+            tile = sb.tile([P, T], U16, name=name)
+            nc.sync.dma_start(out=tile[:].bitcast(I32), in_=words[0].bitcast(I32))
+            return tile
+
+        def load_scales(name, scales):
+            tile = sb.tile([P, T], U8, name=name)
+            nc.vector.memset(tile[:].bitcast(I32), 0)
+            for q in range(4):
+                nc.sync.dma_start(out=tile[32 * q : 32 * q + 4, :].bitcast(I32),
+                                  in_=scales[0, 4 * q : 4 * q + 4, :].bitcast(I32))
+            return tile
+
+        def load(name, src, shape, dtype, queue=nc.sync):
+            tile = sb.tile(shape, dtype, name=name)
+            queue.dma_start(tile[:], src)
+            return tile
+
+        idx = load("idx", offs, [P, J // 16], U16)
+        tab_w = load_words("tab_w", tab_words)
+        tab_s = load_scales("tab_s", tab_scales)
+        w_raw = load("w_raw", w1.rearrange("(p j) r -> p j r", j=PACK), [P, PACK, R], F32)
+        dtab_w = load_words("dtab_w", dtab_words)
+        dtab_s = load_scales("dtab_s", dtab_scales)
+        gain_c = load("gain_c", gain, [P, 1], F32, nc.gpsimd)
+        idx2 = load("idx2", offs2, [P, J // 16], U16)
+        idx3 = load("idx3", offs3, [P, M // 16], U16)
+        og_c = load("og_c", og, [P, 1], F32, nc.gpsimd)
+        pb_t = load("pb_t", pb[0].partition_broadcast(P), [P, M], F32)
+        base_t = load("base_t", base, [P, M], F32)
+
+        pg = sb.tile([P, U], F32)
+        nc.vector.memset(pg[:], 0.0)
+
+        w_bf = sb.tile([P, R, PACK], BF16, align_bytes=64)
+        nc.scalar.copy(out=w_bf[:], in_=w_raw[:].rearrange("p j r -> p r j"))
+
+        def gather(name, window, dtype):
+            tile = sb.tile([P, J], dtype, name=name, align_bytes=64)
+            nc.vector.tensor_copy(tile[:], window[:].indirect(idx[:]))
+            return tile
+
+        tab_wg = gather("tab_wg", tab_w, U16)
+        tab_sg = gather("tab_sg", tab_s, U8)
+
+        w_codes = sb.tile([P, R], U32, align_bytes=64)
+        w_scales = sb.tile([P, R], U8, align_bytes=64)
+        nc.vector.quantize_mx(out=w_codes[:].bitcast(FP8X4), scales=w_scales[:],
+                              in_=w_bf[:].rearrange("p r j -> p (r j)"))
+
+        def product(name, words_g, scales_g):
+            acc = psum.tile([P, J], F32, name=name)
+            nc.tensor.matmul_mx(out=acc[:], lhsT=w_codes[:].bitcast(FP8X4), lhsT_scale=w_scales[:],
+                                rhs=words_g[:].bitcast(FP4X4), rhs_scale=scales_g[:], start=True, stop=True)
+            return acc
+
+        a = product("a", tab_wg, tab_sg)
+        dtab_wg = gather("dtab_wg", dtab_w, U16)
+        dtab_sg = gather("dtab_sg", dtab_s, U8)
+        ta = product("ta", dtab_wg, dtab_sg)
+
+        gain_t = sb.tile([P, J], F32)
+        nc.scalar.activation(gain_t[:], gain_c[:].to_broadcast([P, J]), ACT.Copy)
+        h1 = sb.tile([P, J], F32)
+        nc.scalar.activation(h1[:], a[:], ACT.Tanh)
+        nc.vector.tensor_tensor(pg[:].indirect(idx2[:]), h1[:], gain_t[:], ALU.mult)
+
+        h1_sq = sb.tile([P, J], F32)
+        nc.scalar.activation(h1_sq[:], h1[:], ACT.Square)
+        slope = sb.tile([P, J], F32)
+        nc.scalar.activation(slope[:], h1_sq[:], ACT.Identity, bias=1.0, scale=-1.0)
+        ta_gain = sb.tile([P, J], F32)
+        nc.scalar.activation(ta_gain[:], ta[:], ACT.Copy, scale=gain_c[:])
+        og_half = sb.tile([P, 1], F32)
+        nc.scalar.activation(og_half[:], og_c[:], ACT.Copy, scale=-0.5)
+
+        s = sb.tile([P, M], F32)
+        nc.vector.tensor_tensor(s[:], pg[:].indirect(idx3[:]), pb_t[:], ALU.add)
+        nc.vector.tensor_tensor(pg[:].indirect(idx2[:]), ta_gain[:], slope[:], ALU.mult)
+
+        silu_neg = sb.tile([P, M], F32)
+        nc.scalar.activation(silu_neg[:], s[:], ACT.Silu, scale=-1.0)
+        th = sb.tile([P, M], F32)
+        nc.scalar.activation(th[:], s[:], ACT.Tanh, scale=0.5)
+        neg_sig_og = sb.tile([P, M], F32)
+        nc.scalar.activation(neg_sig_og[:], th[:], ACT.Identity, bias=og_half[:], scale=og_half[:])
+        factor = sb.tile([P, M], F32)
+        nc.vector.scalar_tensor_tensor(factor[:], silu_neg[:], 1.0, neg_sig_og[:], ALU.subtract, ALU.mult)
+
+        scaled = sb.tile([P, M], F32)
+        nc.vector.tensor_tensor(scaled[:], pg[:].indirect(idx3[:]), factor[:], ALU.mult)
+        result = sb.tile([P, M], F32)
+        nc.vector.tensor_tensor(result[:], scaled[:], base_t[:], ALU.add)
+        nc.sync.dma_start(out, result[:])

@@ -39,22 +39,22 @@ def tile_attend_twriteread_kernel(tc, dtab_words, dtab_scales, tab_words, tab_sc
                                   in_=scales[0, 4 * q : 4 * q + 4, :].bitcast(I32))
             return tile
 
-        def load(name, src, shape, dtype, queue=nc.sync):
+        def load(name, src, shape, dtype):
             tile = sb.tile(shape, dtype, name=name)
-            queue.dma_start(tile[:], src)
+            nc.sync.dma_start(tile[:], src)
             return tile
 
         idx = load("idx", offs, [P, J // 16], U16)
         tab_w = load_words("tab_w", tab_words)
         tab_s = load_scales("tab_s", tab_scales)
         w_raw = load("w_raw", w1.rearrange("(p j) r -> p j r", j=PACK), [P, PACK, R], F32)
-        dtab_w = load_words("dtab_w", dtab_words)
+        gain_c = load("gain_c", gain, [P, 1], F32)
         dtab_s = load_scales("dtab_s", dtab_scales)
-        gain_c = load("gain_c", gain, [P, 1], F32, nc.gpsimd)
+        dtab_w = load_words("dtab_w", dtab_words)
         idx2 = load("idx2", offs2, [P, J // 16], U16)
         idx3 = load("idx3", offs3, [P, M // 16], U16)
-        og_c = load("og_c", og, [P, 1], F32, nc.gpsimd)
         pb_t = load("pb_t", pb[0].partition_broadcast(P), [P, M], F32)
+        og_c = load("og_c", og, [P, 1], F32)
         base_t = load("base_t", base, [P, M], F32)
 
         pg = sb.tile([P, U], F32)
@@ -83,8 +83,8 @@ def tile_attend_twriteread_kernel(tc, dtab_words, dtab_scales, tab_words, tab_sc
             return acc
 
         a = product("a", tab_wg, tab_sg)
-        dtab_wg = gather("dtab_wg", dtab_w, U16)
         dtab_sg = gather("dtab_sg", dtab_s, U8)
+        dtab_wg = gather("dtab_wg", dtab_w, U16)
         ta = product("ta", dtab_wg, dtab_sg)
 
         gain_t = sb.tile([P, J], F32)
@@ -99,8 +99,6 @@ def tile_attend_twriteread_kernel(tc, dtab_words, dtab_scales, tab_words, tab_sc
         nc.scalar.activation(slope[:], h1_sq[:], ACT.Identity, bias=1.0, scale=-1.0)
         ta_gain = sb.tile([P, J], F32)
         nc.scalar.activation(ta_gain[:], ta[:], ACT.Copy, scale=gain_c[:])
-        og_half = sb.tile([P, 1], F32)
-        nc.scalar.activation(og_half[:], og_c[:], ACT.Copy, scale=-0.5)
 
         s = sb.tile([P, M], F32)
         nc.vector.tensor_tensor(s[:], pg[:].indirect(idx3[:]), pb_t[:], ALU.add)
@@ -110,13 +108,18 @@ def tile_attend_twriteread_kernel(tc, dtab_words, dtab_scales, tab_words, tab_sc
         nc.scalar.activation(silu_neg[:], s[:], ACT.Silu, scale=-1.0)
         th = sb.tile([P, M], F32)
         nc.scalar.activation(th[:], s[:], ACT.Tanh, scale=0.5)
-        neg_sig_og = sb.tile([P, M], F32)
-        nc.scalar.activation(neg_sig_og[:], th[:], ACT.Identity, bias=og_half[:], scale=og_half[:])
-        factor = sb.tile([P, M], F32)
-        nc.vector.scalar_tensor_tensor(factor[:], silu_neg[:], 1.0, neg_sig_og[:], ALU.subtract, ALU.mult)
-
-        scaled = sb.tile([P, M], F32)
-        nc.vector.tensor_tensor(scaled[:], pg[:].indirect(idx3[:]), factor[:], ALU.mult)
-        result = sb.tile([P, M], F32)
-        nc.vector.tensor_tensor(result[:], scaled[:], base_t[:], ALU.add)
-        nc.sync.dma_start(out, result[:])
+        neg_sig = sb.tile([P, M], F32)
+        nc.scalar.activation(neg_sig[:], th[:], ACT.Identity, bias=-0.5, scale=-0.5)
+        halves = [slice(0, M // 2), slice(M // 2, M)]
+        factor = [sb.tile([P, M // 2], F32, name=f"factor{h}") for h in range(2)]
+        scaled = [sb.tile([P, M // 2], F32, name=f"scaled{h}") for h in range(2)]
+        result = [sb.tile([P, M // 2], F32, name=f"result{h}") for h in range(2)]
+        for h, cols in enumerate(halves):
+            nc.vector.scalar_tensor_tensor(factor[h][:], silu_neg[:, cols], 1.0, neg_sig[:, cols],
+                                           ALU.subtract, ALU.mult)
+        for h, cols in enumerate(halves):
+            picks = idx3[:, cols.start // 16 : cols.stop // 16]
+            nc.vector.tensor_tensor(scaled[h][:], pg[:].indirect(picks), factor[h][:], ALU.mult)
+        for h, (cols, queue) in enumerate(zip(halves, (nc.sync, nc.scalar))):
+            nc.vector.scalar_tensor_tensor(result[h][:], scaled[h][:], og_c[:], base_t[:, cols], ALU.mult, ALU.add)
+            queue.dma_start(out[:, cols], result[h][:])

@@ -1,6 +1,7 @@
 from contextlib import ExitStack
 
 import concourse.mybir as mybir
+from concourse.masks import make_identity
 
 F32 = mybir.dt.float32
 BF16 = mybir.dt.bfloat16
@@ -44,27 +45,31 @@ def tile_attend_twriteread_kernel(tc, dtab_words, dtab_scales, tab_words, tab_sc
             nc.sync.dma_start(tile[:], src)
             return tile
 
-        idx = load("idx", offs, [P, J // 16], U16)
         tab_w = load_words("tab_w", tab_words)
+        idx = load("idx", offs, [P, J // 16], U16)
         tab_s = load_scales("tab_s", tab_scales)
-        w_raw = load("w_raw", w1.rearrange("(p j) r -> p j r", j=PACK), [P, PACK, R], F32)
+        w_raw = sb.tile([P, PACK, R], F32, tag="dtab_wg", align_bytes=64)
+        nc.sync.dma_start(w_raw[:], w1.rearrange("(p j) r -> p j r", j=PACK))
+        dtab_w = load_words("dtab_w", dtab_words)
         gain_c = load("gain_c", gain, [P, 1], F32)
         dtab_s = load_scales("dtab_s", dtab_scales)
-        dtab_w = load_words("dtab_w", dtab_words)
         idx2 = load("idx2", offs2, [P, J // 16], U16)
+        pb_c = load("pb_c", pb.rearrange("o (p c) -> (o p) c", c=2), [P, 2], F32)
         idx3 = load("idx3", offs3, [P, M // 16], U16)
-        pb_t = load("pb_t", pb[0].partition_broadcast(P), [P, M], F32)
         og_c = load("og_c", og, [P, 1], F32)
         base_t = load("base_t", base, [P, M], F32)
 
         pg = sb.tile([P, U], F32)
         nc.vector.memset(pg[:], 0.0)
 
+        ident = sb.tile([P, P], F32)
+        make_identity(nc, ident[:])
+
         w_bf = sb.tile([P, R, PACK], BF16, align_bytes=64)
         nc.scalar.copy(out=w_bf[:], in_=w_raw[:].rearrange("p j r -> p r j"))
 
         def gather(name, window, dtype):
-            tile = sb.tile([P, J], dtype, name=name, align_bytes=64)
+            tile = sb.tile([P, J], dtype, name=name, tag=name, align_bytes=64)
             nc.vector.tensor_copy(tile[:], window[:].indirect(idx[:]))
             return tile
 
@@ -77,14 +82,14 @@ def tile_attend_twriteread_kernel(tc, dtab_words, dtab_scales, tab_words, tab_sc
                               in_=w_bf[:].rearrange("p r j -> p (r j)"))
 
         def product(name, words_g, scales_g):
-            acc = psum.tile([P, J], F32, name=name)
+            acc = psum.tile([P, J], F32, name=name, tag=name)
             nc.tensor.matmul_mx(out=acc[:], lhsT=w_codes[:].bitcast(FP8X4), lhsT_scale=w_scales[:],
                                 rhs=words_g[:].bitcast(FP4X4), rhs_scale=scales_g[:], start=True, stop=True)
             return acc
 
         a = product("a", tab_wg, tab_sg)
-        dtab_sg = gather("dtab_sg", dtab_s, U8)
         dtab_wg = gather("dtab_wg", dtab_w, U16)
+        dtab_sg = gather("dtab_sg", dtab_s, U8)
         ta = product("ta", dtab_wg, dtab_sg)
 
         gain_t = sb.tile([P, J], F32)
@@ -97,6 +102,11 @@ def tile_attend_twriteread_kernel(tc, dtab_words, dtab_scales, tab_words, tab_sc
         nc.scalar.activation(h1_sq[:], h1[:], ACT.Square)
         slope = sb.tile([P, J], F32)
         nc.scalar.activation(slope[:], h1_sq[:], ACT.Identity, bias=1.0, scale=-1.0)
+        pb_ps = psum.tile([P, 2, P], F32, tag="a")
+        for c in range(2):
+            nc.tensor.transpose(pb_ps[:, c, :], pb_c[:, c : c + 1].to_broadcast([P, P]), ident[:])
+        pb_t = sb.tile([P, M], F32)
+        nc.scalar.copy(out=pb_t[:].rearrange("q (p c) -> q p c", c=2), in_=pb_ps[:].rearrange("q c p -> q p c"))
         ta_gain = sb.tile([P, J], F32)
         nc.scalar.activation(ta_gain[:], ta[:], ACT.Copy, scale=gain_c[:])
 

from contextlib import ExitStack

import concourse.mybir as mybir
from concourse.masks import make_identity

F32 = mybir.dt.float32
BF16 = mybir.dt.bfloat16
I32 = mybir.dt.int32
U32 = mybir.dt.uint32
U16 = mybir.dt.uint16
U8 = mybir.dt.uint8
FP8X4 = mybir.dt.float8_e4m3fn_x4
FP4X4 = mybir.dt.float4_e2m1fn_x4
ALU = mybir.AluOpType
ACT = mybir.ActivationFunctionType

P = 128
PACK = 4
K, R, T, J, U, M = 512, 128, 2048, 512, 1024, 256
FLOPS = 2 * 2 * K * R * J


def tile_attend_twriteread_kernel(tc, dtab_words, dtab_scales, tab_words, tab_scales, w1, gain, pb, og, base,
                                   offs, offs2, offs3, out):
    nc = tc.nc
    with ExitStack() as ctx:
        sb = ctx.enter_context(tc.tile_pool(name="sb", bufs=1))
        psum = ctx.enter_context(tc.psum_pool(name="psum", bufs=1))

        def load_words(name, words):
            tile = sb.tile([P, T], U16, name=name)
            nc.sync.dma_start(out=tile[:].bitcast(I32), in_=words[0].bitcast(I32))
            return tile

        def load_scales(name, scales):
            tile = sb.tile([P, T], U8, name=name)
            nc.vector.memset(tile[:].bitcast(I32), 0)
            for q in range(4):
                nc.sync.dma_start(out=tile[32 * q : 32 * q + 4, :].bitcast(I32),
                                  in_=scales[0, 4 * q : 4 * q + 4, :].bitcast(I32))
            return tile

        def load(name, src, shape, dtype):
            tile = sb.tile(shape, dtype, name=name)
            nc.sync.dma_start(tile[:], src)
            return tile

        tab_w = load_words("tab_w", tab_words)
        idx = load("idx", offs, [P, J // 16], U16)
        tab_s = load_scales("tab_s", tab_scales)
        w_raw = sb.tile([P, PACK, R], F32, tag="dtab_wg", align_bytes=64)
        nc.sync.dma_start(w_raw[:], w1.rearrange("(p j) r -> p j r", j=PACK))
        dtab_w = load_words("dtab_w", dtab_words)
        gain_c = load("gain_c", gain, [P, 1], F32)
        dtab_s = load_scales("dtab_s", dtab_scales)
        idx2 = load("idx2", offs2, [P, J // 16], U16)
        pb_c = load("pb_c", pb.rearrange("o (p c) -> (o p) c", c=2), [P, 2], F32)
        idx3 = load("idx3", offs3, [P, M // 16], U16)
        og_c = load("og_c", og, [P, 1], F32)
        base_t = load("base_t", base, [P, M], F32)

        pg = sb.tile([P, U], F32)
        nc.vector.memset(pg[:], 0.0)

        ident = sb.tile([P, P], F32)
        make_identity(nc, ident[:])

        w_bf = sb.tile([P, R, PACK], BF16, align_bytes=64)
        nc.scalar.copy(out=w_bf[:], in_=w_raw[:].rearrange("p j r -> p r j"))

        def gather(name, window, dtype):
            tile = sb.tile([P, J], dtype, name=name, tag=name, align_bytes=64)
            nc.vector.tensor_copy(tile[:], window[:].indirect(idx[:]))
            return tile

        tab_wg = gather("tab_wg", tab_w, U16)
        tab_sg = gather("tab_sg", tab_s, U8)

        w_codes = sb.tile([P, R], U32, align_bytes=64)
        w_scales = sb.tile([P, R], U8, align_bytes=64)
        nc.vector.quantize_mx(out=w_codes[:].bitcast(FP8X4), scales=w_scales[:],
                              in_=w_bf[:].rearrange("p r j -> p (r j)"))

        def product(name, words_g, scales_g):
            acc = psum.tile([P, J], F32, name=name, tag=name)
            nc.tensor.matmul_mx(out=acc[:], lhsT=w_codes[:].bitcast(FP8X4), lhsT_scale=w_scales[:],
                                rhs=words_g[:].bitcast(FP4X4), rhs_scale=scales_g[:], start=True, stop=True)
            return acc

        a = product("a", tab_wg, tab_sg)
        dtab_wg = gather("dtab_wg", dtab_w, U16)
        dtab_sg = gather("dtab_sg", dtab_s, U8)
        ta = product("ta", dtab_wg, dtab_sg)

        gain_t = sb.tile([P, J], F32)
        nc.scalar.activation(gain_t[:], gain_c[:].to_broadcast([P, J]), ACT.Copy)
        h1 = sb.tile([P, J], F32)
        nc.scalar.activation(h1[:], a[:], ACT.Tanh)
        nc.vector.tensor_tensor(pg[:].indirect(idx2[:]), h1[:], gain_t[:], ALU.mult)

        h1_sq = sb.tile([P, J], F32)
        nc.scalar.activation(h1_sq[:], h1[:], ACT.Square)
        slope = sb.tile([P, J], F32)
        nc.scalar.activation(slope[:], h1_sq[:], ACT.Identity, bias=1.0, scale=-1.0)
        pb_ps = psum.tile([P, 2, P], F32, tag="a")
        for c in range(2):
            nc.tensor.transpose(pb_ps[:, c, :], pb_c[:, c : c + 1].to_broadcast([P, P]), ident[:])
        pb_t = sb.tile([P, M], F32)
        nc.scalar.copy(out=pb_t[:].rearrange("q (p c) -> q p c", c=2), in_=pb_ps[:].rearrange("q c p -> q p c"))
        ta_gain = sb.tile([P, J], F32)
        nc.scalar.activation(ta_gain[:], ta[:], ACT.Copy, scale=gain_c[:])

        s = sb.tile([P, M], F32)
        nc.vector.tensor_tensor(s[:], pg[:].indirect(idx3[:]), pb_t[:], ALU.add)
        nc.vector.tensor_tensor(pg[:].indirect(idx2[:]), ta_gain[:], slope[:], ALU.mult)

        silu_neg = sb.tile([P, M], F32)
        nc.scalar.activation(silu_neg[:], s[:], ACT.Silu, scale=-1.0)
        th = sb.tile([P, M], F32)
        nc.scalar.activation(th[:], s[:], ACT.Tanh, scale=0.5)
        neg_sig = sb.tile([P, M], F32)
        nc.scalar.activation(neg_sig[:], th[:], ACT.Identity, bias=-0.5, scale=-0.5)
        halves = [slice(0, M // 2), slice(M // 2, M)]
        factor = [sb.tile([P, M // 2], F32, name=f"factor{h}") for h in range(2)]
        scaled = [sb.tile([P, M // 2], F32, name=f"scaled{h}") for h in range(2)]
        result = [sb.tile([P, M // 2], F32, name=f"result{h}") for h in range(2)]
        for h, cols in enumerate(halves):
            nc.vector.scalar_tensor_tensor(factor[h][:], silu_neg[:, cols], 1.0, neg_sig[:, cols],
                                           ALU.subtract, ALU.mult)
        for h, cols in enumerate(halves):
            picks = idx3[:, cols.start // 16 : cols.stop // 16]
            nc.vector.tensor_tensor(scaled[h][:], pg[:].indirect(picks), factor[h][:], ALU.mult)
        for h, (cols, queue) in enumerate(zip(halves, (nc.sync, nc.scalar))):
            nc.vector.scalar_tensor_tensor(result[h][:], scaled[h][:], og_c[:], base_t[:, cols], ALU.mult, ALU.add)
            queue.dma_start(out[:, cols], result[h][:])
